import numpy as np
import ml_dtypes


def mxq(x, axis, fmt="e4m3"):
    dtype, down = {"e4m3": (ml_dtypes.float8_e4m3fn, 7), "e5m2": (ml_dtypes.float8_e5m2, 14)}[fmt]
    v = np.moveaxis(np.asarray(x, np.float32).astype(ml_dtypes.bfloat16).astype(np.float64), axis, -1)
    blocks = v.reshape(v.shape[:-1] + (-1, 32))
    amax = np.abs(blocks).max(-1, keepdims=True)
    byte = np.maximum(np.where(amax > 0, np.frexp(amax)[1] - 1 + 127, 0) - down, 1)
    scale = np.exp2(byte - 127.0)
    codes = (blocks / scale).astype(np.float32).astype(dtype).astype(np.float64)
    return np.moveaxis((codes * scale).reshape(v.shape), -1, axis)


WIDE = False


def mx_kscale(k):
    if not WIDE:
        return np.ones(k)
    levels = np.array([10, -10, 5, -5, 0])
    if k % 512:
        return np.exp2(np.random.permutation(np.resize(levels, k // 32))).repeat(32)
    a = np.empty((k // 512, 16))
    for p in range(k // 512):
        a[p, :8] = np.random.permutation(np.resize(levels, 8))
        for g in range(8):
            far = levels[np.abs(levels - a[p, g]) >= 10]
            a[p, g + 8] = far[np.random.randint(len(far))]
    return np.exp2(a.ravel()).repeat(32)


def f64(x):
    return np.asarray(x).astype(np.float64)


def striped(idx):
    return np.tile(idx.reshape(-1, 16).T, (8, 1)).astype(np.uint16)


def unstriped(offs):
    return offs[:16].T.reshape(-1).astype(np.int64)


E2M1 = np.array([0.0, 0.5, 1.0, 1.5, 2.0, 3.0, 4.0, 6.0, -0.0, -0.5, -1.0, -1.5, -2.0, -3.0, -4.0, -6.0])


def pack_weight(w, fmt):
    k, n = w.shape
    w = f64(np.asarray(w, np.float32).astype(ml_dtypes.bfloat16)).reshape(k // 32, 32, n)
    amax = np.abs(w).max(1)
    if fmt == "e4m3":
        byte = np.frexp(amax)[1] - 1 + 127 - 7
    else:
        mant, ex = np.frexp(amax / 6.0)
        byte = np.where(mant > 0.5, ex, ex - 1) + 127
    byte = np.clip(np.where(amax > 0, byte, 1), 1, 254)
    scaled = (w * np.exp2(127.0 - byte)[:, None, :]).reshape(k, n).astype(np.float32)
    by_word = np.ascontiguousarray(scaled.reshape(k // 512, 128, 4, n).transpose(0, 1, 3, 2))
    if fmt == "e4m3":
        words = by_word.astype(ml_dtypes.float8_e4m3fn).view(np.uint8)
    else:
        c = by_word.astype(ml_dtypes.float4_e2m1fn).view(np.uint8) & 0xF
        words = (c[..., 0::2] | (c[..., 1::2] << 4)).reshape(k // 512, 128, 2 * n)
    return np.ascontiguousarray(words), np.ascontiguousarray(byte.astype(np.uint8).reshape(k // 512, 16, n))


def unpack_weight(words, scales, fmt):
    g, _, n = scales.shape
    words = np.ascontiguousarray(words).reshape(g, 128, n, -1)
    if fmt == "e4m3":
        vals = words.view(ml_dtypes.float8_e4m3fn).astype(np.float64)
    else:
        nib = np.empty((g, 128, n, 4), np.uint8)
        nib[..., 0::2] = words & 0xF
        nib[..., 1::2] = words >> 4
        vals = E2M1[nib]
    vals = vals * np.repeat(np.exp2(scales.astype(np.float64) - 127.0), 8, axis=1)[..., None]
    return vals.transpose(0, 1, 3, 2).reshape(g * 512, n)


def pack_table(v):
    words, scales = pack_weight(v, "e4m3")
    return np.concatenate([words.reshape(words.shape[0], -1), scales.reshape(scales.shape[0], -1)], axis=1)


def unpack_table(tab):
    g, t = tab.shape[0], tab.shape[1] // 528
    return unpack_weight(tab[:, :512 * t].reshape(g, 128, t, 4), tab[:, 512 * t:].reshape(g, 16, t), "e4m3")


K, M, T, S = 2048, 128, 2048, 1024


def setup_inputs():
    n = np.random.standard_normal
    s = mx_kscale(K)[:, None]
    w = n((K, M)) / np.sqrt(K) / s
    p_w4 = pack_weight(w[512:], "e2m1")
    return {
        "tab": pack_table(n((K, T)) * s),
        "w8": (w[:512]).astype(np.float32),
        "w4_words": p_w4[0],
        "w4_scales": p_w4[1],
        "b": (0.3 * n(128)).astype(np.float32),
        "wgo": np.tile(np.random.uniform(0.5, 2.0, S), (128, 1)).astype(np.float32),
        "offs": striped(np.random.permutation(T)[:S]),
        "offs2": striped(np.random.permutation(T)[:S]),
    }


def reference(tab, w8, w4_words, w4_scales, b, wgo, offs, offs2):
    tab_ = unpack_table(tab)[:, unstriped(offs)]
    w8_ = mxq(f64(w8), 0, "e4m3")
    w4_ = unpack_weight(w4_words, w4_scales, "e2m1")
    y = w8_.T @ tab_[:512] + w4_.T @ tab_[512:]
    out = np.zeros((M, T))
    out[:, unstriped(offs2)] = f64(wgo)[0] * (y + f64(b)[:, None])
    return out

@@ -1,0 +1,127 @@
+from contextlib import ExitStack
+
+import concourse.mybir as mybir
+
+K, M, T, S = 2048, 128, 2048, 1024
+FLOPS = 2 * K * M * S
+
+F32 = mybir.dt.float32
+BF16 = mybir.dt.bfloat16
+I32 = mybir.dt.int32
+U32 = mybir.dt.uint32
+U16 = mybir.dt.uint16
+U8 = mybir.dt.uint8
+FP8X4 = mybir.dt.float8_e4m3fn_x4
+FP4X4 = mybir.dt.float4_e2m1fn_x4
+MULT = mybir.AluOpType.mult
+IDENTITY = mybir.ActivationFunctionType.Identity
+
+P = 128
+PASSES = K // 512
+FIRST = 384
+ROW0 = 32
+
+
+def tile_list_tabscat_o_bias_kernel(tc, tab, w8, w4_words, w4_scales, b, wgo, offs, offs2, out):
+    nc = tc.nc
+    with ExitStack() as ctx:
+        pool = ctx.enter_context(tc.tile_pool(name="keep", bufs=1))
+        psum = ctx.enter_context(tc.psum_pool(name="psum", bufs=1))
+
+        pick = pool.tile([P, S // 16], U16, name="pick")
+        place = pool.tile([P, S // 16], U16, name="place")
+        scale_rows = pool.tile([P, T], U8, name="scale_rows", align_bytes=64)
+        picked_rows = pool.tile([P, S], U8, name="picked_rows", align_bytes=64)
+        planes = pool.tile([P, PASSES * S], U8, name="planes", align_bytes=64)
+        words = [pool.tile([P, T], I32, name="words%d" % a, align_bytes=64) for a in range(PASSES)]
+        picked = [pool.tile([P, S], U32, name="picked%d" % a, align_bytes=64) for a in range(PASSES)]
+        w8_raw = pool.tile([P, 4, M], F32, name="w8_raw")
+        w8_bf = pool.tile([P, M, 4], BF16, name="w8_bf", align_bytes=64)
+        w8_codes = pool.tile([P, M], U32, name="w8_codes", align_bytes=64)
+        w8_plane = pool.tile([P, M], U8, name="w8_plane", align_bytes=64)
+        w4_codes = pool.tile([P, PASSES - 1, 2 * M], U8, name="w4_codes", align_bytes=64)
+        w4_planes = pool.tile([P, PASSES - 1, M], U8, name="w4_planes", align_bytes=64)
+        bias = pool.tile([P, 1], F32, name="bias")
+        gain = pool.tile([P, S], F32, name="gain")
+        page = pool.tile([P, T], F32, name="page")
+
+        nc.sync.dma_start(pick[:], offs)
+        nc.sync.dma_start(
+            scale_rows[ROW0 : ROW0 + 64, :].bitcast(I32),
+            tab[:, 512 * T :].rearrange("a (q t) -> q a t", q=16).bitcast(I32),
+        )
+
+        def load_words(a):
+            nc.sync.dma_start(words[a][:], tab[a, : 512 * T].rearrange("(p c) -> p c", p=P).bitcast(I32))
+
+        load_words(0)
+        nc.sync.dma_start(w8_raw[:], w8.rearrange("(p j) n -> p j n", j=4))
+        for a in range(1, PASSES):
+            load_words(a)
+        nc.sync.dma_start(place[:], offs2)
+        nc.sync.dma_start(gain[:], wgo)
+
+        nc.vector.memset(scale_rows[:ROW0, :].bitcast(I32), 0)
+        nc.vector.memset(scale_rows[ROW0 + 64 :, :].bitcast(I32), 0)
+        nc.vector.memset(planes[:].bitcast(I32), 0)
+
+        nc.gpsimd.memset(w4_planes[:].rearrange("p a n -> p (a n)").bitcast(I32), 0)
+        for quad in range(4):
+            nc.gpsimd.dma_start(
+                w4_planes[32 * quad : 32 * quad + 4, :, :].bitcast(I32),
+                w4_scales[:, 4 * quad : 4 * quad + 4, :].rearrange("a r n -> r a n").bitcast(I32),
+            )
+        nc.gpsimd.dma_start(w4_codes[:].bitcast(I32), w4_words.rearrange("a p c -> p a c").bitcast(I32))
+        nc.gpsimd.dma_start(bias[:], b.rearrange("(p o) -> p o", o=1))
+        nc.gpsimd.memset(page[:], 0.0)
+
+        nc.vector.tensor_copy(picked_rows[:], scale_rows[:].indirect(pick[:]))
+        for quad in range(4):
+            nc.scalar.dma_start(
+                planes[32 * quad : 32 * quad + 4, :].bitcast(I32),
+                picked_rows[ROW0 + 16 * quad : ROW0 + 16 * quad + 16, :].bitcast(I32),
+            )
+
+        nc.scalar.copy(w8_bf[:], w8_raw[:].rearrange("p j n -> p n j"))
+
+        nc.vector.tensor_copy(picked[0][:], words[0][:].bitcast(U32).indirect(pick[:]))
+        nc.vector.quantize_mx(
+            out=w8_codes[:].bitcast(FP8X4), scales=w8_plane[:], in_=w8_bf[:].rearrange("p n j -> p (n j)")
+        )
+        for a in range(1, PASSES - 1):
+            nc.vector.tensor_copy(picked[a][:], words[a][:].bitcast(U32).indirect(pick[:]))
+        last = PASSES - 1
+        parts = [(0, FIRST), (FIRST, S)]
+        for lo, hi in parts:
+            nc.vector.tensor_copy(
+                picked[last][:, lo:hi], words[last][:].bitcast(U32).indirect(pick[:, lo // 16 : hi // 16])
+            )
+
+        banks = [(0, 384, 128), (384, 512, 512), (896, 128, 128)]
+        sums = [pool.tile([P, hi - lo], F32, name="sums%d" % lo) for lo, hi in parts]
+        accs = [psum.tile([P, n], F32, name="acc%d" % lo) for lo, n, width in banks]
+        for a in range(PASSES):
+            if a == 0:
+                codes, plane = w8_codes[:].bitcast(FP8X4), w8_plane[:]
+            else:
+                codes, plane = w4_codes[:, a - 1, :].bitcast(FP4X4), w4_planes[:, a - 1, :]
+            for acc, (lo, n, width) in zip(accs, banks):
+                for c in range(0, n, width):
+                    nc.tensor.matmul_mx(
+                        out=acc[:, c : c + width],
+                        lhsT=codes,
+                        lhsT_scale=plane,
+                        rhs=picked[a][:, lo + c : lo + c + width].bitcast(FP8X4),
+                        rhs_scale=planes[:, a * S + lo + c : a * S + lo + c + width],
+                        start=(a == 0 and c == 0),
+                        stop=(a == last and c + width == n),
+                    )
+        for acc, (lo, n, width) in zip(accs, banks):
+            part = 0 if lo < FIRST else 1
+            at = lo - parts[part][0]
+            nc.scalar.activation(sums[part][:, at : at + n], acc[:], IDENTITY, bias=bias[:])
+        for part, (lo, hi) in enumerate(parts):
+            nc.vector.tensor_tensor(
+                page[:].indirect(place[:, lo // 16 : hi // 16]), sums[part][:], gain[:, lo:hi], MULT
+            )
+        nc.sync.dma_start(out, page[:])

@@ -19,7 +19,7 @@ IDENTITY = mybir.ActivationFunctionType.Identity
 P = 128
 PASSES = K // 512
 FIRST = 384
-ROW0 = 32
+SHIFTED = 112
 
 
 def tile_list_tabscat_o_bias_kernel(tc, tab, w8, w4_words, w4_scales, b, wgo, offs, offs2, out):
@@ -32,62 +32,63 @@ def tile_list_tabscat_o_bias_kernel(tc, tab, w8, w4_words, w4_scales, b, wgo, of
         place = pool.tile([P, S // 16], U16, name="place")
         scale_rows = pool.tile([P, T], U8, name="scale_rows", align_bytes=64)
         picked_rows = pool.tile([P, S], U8, name="picked_rows", align_bytes=64)
-        planes = pool.tile([P, PASSES * S], U8, name="planes", align_bytes=64)
-        words = [pool.tile([P, T], I32, name="words%d" % a, align_bytes=64) for a in range(PASSES)]
+        planes = [picked_rows] + [pool.tile([P, S], U8, name="plane%d" % a, align_bytes=64) for a in range(1, PASSES)]
+        words = [pool.tile([P, T], I32, name="words%d" % a, tag="words%d" % a, align_bytes=64) for a in range(PASSES)]
         picked = [pool.tile([P, S], U32, name="picked%d" % a, align_bytes=64) for a in range(PASSES)]
-        w8_raw = pool.tile([P, 4, M], F32, name="w8_raw")
+        w8_raw = pool.tile([P, 4, M], F32, name="w8_raw", tag="w8_raw")
         w8_bf = pool.tile([P, M, 4], BF16, name="w8_bf", align_bytes=64)
         w8_codes = pool.tile([P, M], U32, name="w8_codes", align_bytes=64)
         w8_plane = pool.tile([P, M], U8, name="w8_plane", align_bytes=64)
         w4_codes = pool.tile([P, PASSES - 1, 2 * M], U8, name="w4_codes", align_bytes=64)
         w4_planes = pool.tile([P, PASSES - 1, M], U8, name="w4_planes", align_bytes=64)
-        bias = pool.tile([P, 1], F32, name="bias")
-        gain = pool.tile([P, S], F32, name="gain")
         page = pool.tile([P, T], F32, name="page")
 
+        warm = pool.tile([P, 16], F32, name="warm")
+        nc.vector.memset(scale_rows[:].bitcast(I32), 0)
+        nc.vector.memset(warm[:, :8], 0.0)
+        nc.scalar.activation(warm[:, 8:], warm[:, :8], IDENTITY)
+        nc.vector.memset(page[:], 0.0)
+
         nc.sync.dma_start(pick[:], offs)
-        nc.sync.dma_start(
-            scale_rows[ROW0 : ROW0 + 64, :].bitcast(I32),
-            tab[:, 512 * T :].rearrange("a (q t) -> q a t", q=16).bitcast(I32),
-        )
+        nc.sync.dma_start(w8_raw[:], w8.rearrange("(p j) n -> p j n", j=4))
+        tab_scales = tab[:, 512 * T :].rearrange("a (q t) -> a q t", q=16)
+        for quad in range(4):
+            nc.sync.dma_start(
+                scale_rows[32 * quad : 32 * quad + 16, :].bitcast(I32),
+                tab_scales[:, 4 * quad : 4 * quad + 4, :].bitcast(I32),
+            )
 
         def load_words(a):
             nc.sync.dma_start(words[a][:], tab[a, : 512 * T].rearrange("(p c) -> p c", p=P).bitcast(I32))
 
         load_words(0)
-        nc.sync.dma_start(w8_raw[:], w8.rearrange("(p j) n -> p j n", j=4))
-        for a in range(1, PASSES):
-            load_words(a)
+        load_words(1)
+        load_words(2)
+        load_words(3)
         nc.sync.dma_start(place[:], offs2)
+        gain = pool.tile([P, S], F32, name="gain")
         nc.sync.dma_start(gain[:], wgo)
 
-        nc.vector.memset(scale_rows[:ROW0, :].bitcast(I32), 0)
-        nc.vector.memset(scale_rows[ROW0 + 64 :, :].bitcast(I32), 0)
-        nc.vector.memset(planes[:].bitcast(I32), 0)
-
-        nc.gpsimd.memset(w4_planes[:].rearrange("p a n -> p (a n)").bitcast(I32), 0)
+        bias = pool.tile([P, 1], F32, name="bias")
+        nc.gpsimd.dma_start(bias[:], b.rearrange("(p o) -> p o", o=1))
         for quad in range(4):
             nc.gpsimd.dma_start(
                 w4_planes[32 * quad : 32 * quad + 4, :, :].bitcast(I32),
                 w4_scales[:, 4 * quad : 4 * quad + 4, :].rearrange("a r n -> r a n").bitcast(I32),
             )
         nc.gpsimd.dma_start(w4_codes[:].bitcast(I32), w4_words.rearrange("a p c -> p a c").bitcast(I32))
-        nc.gpsimd.dma_start(bias[:], b.rearrange("(p o) -> p o", o=1))
-        nc.gpsimd.memset(page[:], 0.0)
-
-        nc.vector.tensor_copy(picked_rows[:], scale_rows[:].indirect(pick[:]))
-        for quad in range(4):
-            nc.scalar.dma_start(
-                planes[32 * quad : 32 * quad + 4, :].bitcast(I32),
-                picked_rows[ROW0 + 16 * quad : ROW0 + 16 * quad + 16, :].bitcast(I32),
-            )
 
         nc.scalar.copy(w8_bf[:], w8_raw[:].rearrange("p j n -> p n j"))
-
-        nc.vector.tensor_copy(picked[0][:], words[0][:].bitcast(U32).indirect(pick[:]))
         nc.vector.quantize_mx(
             out=w8_codes[:].bitcast(FP8X4), scales=w8_plane[:], in_=w8_bf[:].rearrange("p n j -> p (n j)")
         )
+
+        nc.vector.tensor_copy(picked_rows[:], scale_rows[:].indirect(pick[:]))
+        for a in range(1, PASSES):
+            nc.scalar.dma_start(planes[a][:SHIFTED, :].bitcast(I32), picked_rows[4 * a : 4 * a + SHIFTED, :].bitcast(I32))
+
+
+        nc.vector.tensor_copy(picked[0][:], words[0][:].bitcast(U32).indirect(pick[:]))
         for a in range(1, PASSES - 1):
             nc.vector.tensor_copy(picked[a][:], words[a][:].bitcast(U32).indirect(pick[:]))
         last = PASSES - 1
@@ -112,7 +113,7 @@ def tile_list_tabscat_o_bias_kernel(tc, tab, w8, w4_words, w4_scales, b, wgo, of
                         lhsT=codes,
                         lhsT_scale=plane,
                         rhs=picked[a][:, lo + c : lo + c + width].bitcast(FP8X4),
-                        rhs_scale=planes[:, a * S + lo + c : a * S + lo + c + width],
+                        rhs_scale=planes[a][:, lo + c : lo + c + width],
                         start=(a == 0 and c == 0),
                         stop=(a == last and c + width == n),
                     )

from contextlib import ExitStack

import concourse.mybir as mybir

K, M, T, S = 2048, 128, 2048, 1024
FLOPS = 2 * K * M * S

F32 = mybir.dt.float32
BF16 = mybir.dt.bfloat16
I32 = mybir.dt.int32
U32 = mybir.dt.uint32
U16 = mybir.dt.uint16
U8 = mybir.dt.uint8
FP8X4 = mybir.dt.float8_e4m3fn_x4
FP4X4 = mybir.dt.float4_e2m1fn_x4
MULT = mybir.AluOpType.mult
IDENTITY = mybir.ActivationFunctionType.Identity

P = 128
PASSES = K // 512
FIRST = 384
SHIFTED = 112


def tile_list_tabscat_o_bias_kernel(tc, tab, w8, w4_words, w4_scales, b, wgo, offs, offs2, out):
    nc = tc.nc
    with ExitStack() as ctx:
        pool = ctx.enter_context(tc.tile_pool(name="keep", bufs=1))
        psum = ctx.enter_context(tc.psum_pool(name="psum", bufs=1))

        pick = pool.tile([P, S // 16], U16, name="pick")
        place = pool.tile([P, S // 16], U16, name="place")
        scale_rows = pool.tile([P, T], U8, name="scale_rows", align_bytes=64)
        picked_rows = pool.tile([P, S], U8, name="picked_rows", align_bytes=64)
        planes = [picked_rows] + [pool.tile([P, S], U8, name="plane%d" % a, align_bytes=64) for a in range(1, PASSES)]
        words = [pool.tile([P, T], I32, name="words%d" % a, tag="words%d" % a, align_bytes=64) for a in range(PASSES)]
        picked = [pool.tile([P, S], U32, name="picked%d" % a, align_bytes=64) for a in range(PASSES)]
        w8_raw = pool.tile([P, 4, M], F32, name="w8_raw", tag="w8_raw")
        w8_bf = pool.tile([P, M, 4], BF16, name="w8_bf", align_bytes=64)
        w8_codes = pool.tile([P, M], U32, name="w8_codes", align_bytes=64)
        w8_plane = pool.tile([P, M], U8, name="w8_plane", align_bytes=64)
        w4_codes = pool.tile([P, PASSES - 1, 2 * M], U8, name="w4_codes", align_bytes=64)
        w4_planes = pool.tile([P, PASSES - 1, M], U8, name="w4_planes", align_bytes=64)
        page = pool.tile([P, T], F32, name="page")

        warm = pool.tile([P, 16], F32, name="warm")
        nc.vector.memset(scale_rows[:].bitcast(I32), 0)
        nc.vector.memset(warm[:, :8], 0.0)
        nc.scalar.activation(warm[:, 8:], warm[:, :8], IDENTITY)
        nc.vector.memset(page[:], 0.0)

        nc.sync.dma_start(pick[:], offs)
        nc.sync.dma_start(w8_raw[:], w8.rearrange("(p j) n -> p j n", j=4))
        tab_scales = tab[:, 512 * T :].rearrange("a (q t) -> a q t", q=16)
        for quad in range(4):
            nc.sync.dma_start(
                scale_rows[32 * quad : 32 * quad + 16, :].bitcast(I32),
                tab_scales[:, 4 * quad : 4 * quad + 4, :].bitcast(I32),
            )

        def load_words(a):
            nc.sync.dma_start(words[a][:], tab[a, : 512 * T].rearrange("(p c) -> p c", p=P).bitcast(I32))

        load_words(0)
        load_words(1)
        load_words(2)
        load_words(3)
        nc.sync.dma_start(place[:], offs2)
        gain = pool.tile([P, S], F32, name="gain")
        nc.sync.dma_start(gain[:], wgo)

        bias = pool.tile([P, 1], F32, name="bias")
        nc.gpsimd.dma_start(bias[:], b.rearrange("(p o) -> p o", o=1))
        for quad in range(4):
            nc.gpsimd.dma_start(
                w4_planes[32 * quad : 32 * quad + 4, :, :].bitcast(I32),
                w4_scales[:, 4 * quad : 4 * quad + 4, :].rearrange("a r n -> r a n").bitcast(I32),
            )
        nc.gpsimd.dma_start(w4_codes[:].bitcast(I32), w4_words.rearrange("a p c -> p a c").bitcast(I32))

        nc.scalar.copy(w8_bf[:], w8_raw[:].rearrange("p j n -> p n j"))
        nc.vector.quantize_mx(
            out=w8_codes[:].bitcast(FP8X4), scales=w8_plane[:], in_=w8_bf[:].rearrange("p n j -> p (n j)")
        )

        nc.vector.tensor_copy(picked_rows[:], scale_rows[:].indirect(pick[:]))
        for a in range(1, PASSES):
            nc.scalar.dma_start(planes[a][:SHIFTED, :].bitcast(I32), picked_rows[4 * a : 4 * a + SHIFTED, :].bitcast(I32))


        nc.vector.tensor_copy(picked[0][:], words[0][:].bitcast(U32).indirect(pick[:]))
        for a in range(1, PASSES - 1):
            nc.vector.tensor_copy(picked[a][:], words[a][:].bitcast(U32).indirect(pick[:]))
        last = PASSES - 1
        parts = [(0, FIRST), (FIRST, S)]
        for lo, hi in parts:
            nc.vector.tensor_copy(
                picked[last][:, lo:hi], words[last][:].bitcast(U32).indirect(pick[:, lo // 16 : hi // 16])
            )

        banks = [(0, 384, 128), (384, 512, 512), (896, 128, 128)]
        sums = [pool.tile([P, hi - lo], F32, name="sums%d" % lo) for lo, hi in parts]
        accs = [psum.tile([P, n], F32, name="acc%d" % lo) for lo, n, width in banks]
        for a in range(PASSES):
            if a == 0:
                codes, plane = w8_codes[:].bitcast(FP8X4), w8_plane[:]
            else:
                codes, plane = w4_codes[:, a - 1, :].bitcast(FP4X4), w4_planes[:, a - 1, :]
            for acc, (lo, n, width) in zip(accs, banks):
                for c in range(0, n, width):
                    nc.tensor.matmul_mx(
                        out=acc[:, c : c + width],
                        lhsT=codes,
                        lhsT_scale=plane,
                        rhs=picked[a][:, lo + c : lo + c + width].bitcast(FP8X4),
                        rhs_scale=planes[a][:, lo + c : lo + c + width],
                        start=(a == 0 and c == 0),
                        stop=(a == last and c + width == n),
                    )
        for acc, (lo, n, width) in zip(accs, banks):
            part = 0 if lo < FIRST else 1
            at = lo - parts[part][0]
            nc.scalar.activation(sums[part][:, at : at + n], acc[:], IDENTITY, bias=bias[:])
        for part, (lo, hi) in enumerate(parts):
            nc.vector.tensor_tensor(
                page[:].indirect(place[:, lo // 16 : hi // 16]), sums[part][:], gain[:, lo:hi], MULT
            )
        nc.sync.dma_start(out, page[:])
